import numpy as np
import ml_dtypes


def mxq(x, axis, fmt="e4m3"):
    dtype, down = {"e4m3": (ml_dtypes.float8_e4m3fn, 7), "e5m2": (ml_dtypes.float8_e5m2, 14)}[fmt]
    v = np.moveaxis(np.asarray(x, np.float32).astype(ml_dtypes.bfloat16).astype(np.float64), axis, -1)
    blocks = v.reshape(v.shape[:-1] + (-1, 32))
    amax = np.abs(blocks).max(-1, keepdims=True)
    byte = np.maximum(np.where(amax > 0, np.frexp(amax)[1] - 1 + 127, 0) - down, 1)
    scale = np.exp2(byte - 127.0)
    codes = (blocks / scale).astype(np.float32).astype(dtype).astype(np.float64)
    return np.moveaxis((codes * scale).reshape(v.shape), -1, axis)


WIDE = False


def mx_kscale(k):
    if not WIDE:
        return np.ones(k)
    levels = np.array([10, -10, 5, -5, 0])
    if k % 512:
        return np.exp2(np.random.permutation(np.resize(levels, k // 32))).repeat(32)
    a = np.empty((k // 512, 16))
    for p in range(k // 512):
        a[p, :8] = np.random.permutation(np.resize(levels, 8))
        for g in range(8):
            far = levels[np.abs(levels - a[p, g]) >= 10]
            a[p, g + 8] = far[np.random.randint(len(far))]
    return np.exp2(a.ravel()).repeat(32)


def f64(x):
    return np.asarray(x).astype(np.float64)


def striped(idx):
    return np.tile(idx.reshape(-1, 16).T, (8, 1)).astype(np.uint16)


def unstriped(offs):
    return offs[:16].T.reshape(-1).astype(np.int64)


def pack_weight(w):
    k, n = w.shape
    w = f64(np.asarray(w, np.float32).astype(ml_dtypes.bfloat16)).reshape(k // 32, 32, n)
    amax = np.abs(w).max(1)
    byte = np.clip(np.where(amax > 0, np.frexp(amax)[1] - 1 + 127 - 7, 1), 1, 254)
    scaled = (w * np.exp2(127.0 - byte)[:, None, :]).reshape(k, n).astype(np.float32)
    words = np.ascontiguousarray(scaled.reshape(k // 512, 128, 4, n).transpose(0, 1, 3, 2)).astype(ml_dtypes.float8_e4m3fn).view(np.uint8)
    return words, np.ascontiguousarray(byte.astype(np.uint8).reshape(k // 512, 16, n))


def unpack_weight(words, scales):
    g, p, n, _ = words.shape
    vals = np.ascontiguousarray(words).view(ml_dtypes.float8_e4m3fn).astype(np.float64) * np.repeat(np.exp2(scales.astype(np.float64) - 127.0), 8, axis=1)[..., None]
    return vals.transpose(0, 1, 3, 2).reshape(g * 512, n)


K, T, S, N = 512, 1024, 512, 128
P = 2 ** 7


def setup_inputs():
    n = np.random.standard_normal
    s = mx_kscale(K)[:, None]
    packed_xT = pack_weight(n((K, T)) * s)
    return {
        "x_words": packed_xT[0],
        "x_scales": packed_xT[1],
        "zp": np.tile(np.random.uniform(-0.6, 0.6, T), (P, 1)).astype(np.float32),
        "csum": n((N, 1)).astype(np.float32),
        "w1": (n((K, N)) / np.sqrt(K) / s).astype(np.float32),
        "offs": striped(np.random.permutation(T)[:S]),
    }


def reference(x_words, x_scales, zp, csum, w1, offs):
    xq = unpack_weight(x_words, x_scales)[:, unstriped(offs)]
    y = mxq(f64(w1), 0, "e4m3").T @ xq
    zg = f64(zp)[:1][:, unstriped(offs)]
    return y - (f64(csum) * zg)

@@ -1,0 +1,70 @@
+from contextlib import ExitStack
+
+import concourse.mybir as mybir
+
+K, T, S, N = 512, 1024, 512, 128
+FLOPS = 2 * K * S * N
+
+F32 = mybir.dt.float32
+BF16 = mybir.dt.bfloat16
+I32 = mybir.dt.int32
+U32 = mybir.dt.uint32
+U16 = mybir.dt.uint16
+U8 = mybir.dt.uint8
+FP8X4 = mybir.dt.float8_e4m3fn_x4
+ALU = mybir.AluOpType
+
+P = 128
+PACK = 4
+HALF = S // 2
+
+
+def tile_picked_zeropt_none_p_kernel(tc, x_words, x_scales, zp, csum, w1, offs, out):
+    nc = tc.nc
+    with ExitStack() as ctx:
+        pool = ctx.enter_context(tc.tile_pool(name="held", bufs=1))
+        psum = ctx.enter_context(tc.psum_pool(name="psum", bufs=1))
+
+        offsets = pool.tile([P, S // 16], U16, name="offsets")
+        words = pool.tile([P, T], I32, name="words", align_bytes=64)
+        planes = pool.tile([P, T], U8, name="planes", align_bytes=64)
+        zp_all = pool.tile([P, T], F32, name="zp_all", align_bytes=64)
+        w_raw = pool.tile([P, PACK, N], F32, name="w_raw", align_bytes=64)
+        csum_col = pool.tile([P, 1], F32, name="csum_col")
+        csum_neg = pool.tile([P, 1], F32, name="csum_neg")
+
+        nc.vector.memset(planes[:].bitcast(I32), 0)
+        nc.sync.dma_start(offsets[:], offs)
+        nc.scalar.dma_start(words[:], x_words[0].rearrange("p t r -> p (t r)").bitcast(I32))
+        for q in range(4):
+            nc.sync.dma_start(planes[32 * q : 32 * q + 4, :].bitcast(I32), x_scales[0, 4 * q : 4 * q + 4, :].bitcast(I32))
+        nc.scalar.dma_start(w_raw[:], w1.rearrange("(p j) n -> p j n", j=PACK))
+        nc.scalar.dma_start(zp_all[:], zp)
+        nc.gpsimd.dma_start(csum_col[:], csum)
+        nc.gpsimd.tensor_scalar(csum_neg[:], csum_col[:], -1.0, 0.0, ALU.mult, ALU.add)
+
+        x_plane = pool.tile([P, S], U8, name="x_plane", align_bytes=64)
+        nc.vector.tensor_copy(x_plane[:], planes[:].indirect(offsets[:]))
+        x_codes = pool.tile([P, S], U32, name="x_codes", align_bytes=64)
+        nc.vector.tensor_copy(x_codes[:], words[:].bitcast(U32).indirect(offsets[:]))
+
+        w_grouped = pool.tile([P, N, PACK], BF16, name="w_grouped", align_bytes=64)
+        nc.scalar.copy(w_grouped[:], w_raw[:].rearrange("p j n -> p n j"))
+        w_codes = pool.tile([P, N], U32, name="w_codes", align_bytes=64)
+        w_plane = pool.tile([P, N], U8, name="w_plane", align_bytes=64)
+        nc.vector.quantize_mx(out=w_codes[:].bitcast(FP8X4), scales=w_plane[:], in_=w_grouped[:].rearrange("p n j -> p (n j)"))
+
+        acc = psum.tile([N, S], F32, name="acc")
+        nc.tensor.matmul_mx(out=acc[:], lhsT=w_codes[:].bitcast(FP8X4), lhsT_scale=w_plane[:],
+                            rhs=x_codes[:].bitcast(FP8X4), rhs_scale=x_plane[:], start=True, stop=True)
+
+        picked = []
+        for h in range(2):
+            zg = pool.tile([P, HALF], F32, name=f"zg{h}", align_bytes=64)
+            nc.vector.tensor_copy(zg[:], zp_all[:].indirect(offsets[:, h * HALF // 16 : (h + 1) * HALF // 16]))
+            picked.append(zg)
+        for h in range(2):
+            cols = slice(h * HALF, (h + 1) * HALF)
+            res = pool.tile([P, HALF], F32, name=f"res{h}", align_bytes=64)
+            nc.vector.scalar_tensor_tensor(res[:], picked[h][:], csum_neg[:], acc[:, cols], ALU.mult, ALU.add)
+            (nc.sync, nc.scalar)[h].dma_start(out[:, cols], res[:])

@@ -33,13 +33,13 @@ def tile_picked_zeropt_none_p_kernel(tc, x_words, x_scales, zp, csum, w1, offs, 
         csum_col = pool.tile([P, 1], F32, name="csum_col")
         csum_neg = pool.tile([P, 1], F32, name="csum_neg")
 
-        nc.vector.memset(planes[:].bitcast(I32), 0)
         nc.sync.dma_start(offsets[:], offs)
-        nc.scalar.dma_start(words[:], x_words[0].rearrange("p t r -> p (t r)").bitcast(I32))
         for q in range(4):
-            nc.sync.dma_start(planes[32 * q : 32 * q + 4, :].bitcast(I32), x_scales[0, 4 * q : 4 * q + 4, :].bitcast(I32))
-        nc.scalar.dma_start(w_raw[:], w1.rearrange("(p j) n -> p j n", j=PACK))
-        nc.scalar.dma_start(zp_all[:], zp)
+            rows = x_scales[0, 4 * q : 4 * q + 4, :].bitcast(I32)
+            (nc.scalar, nc.sync)[q // 2].dma_start(planes[32 * q : 32 * q + 32, :].bitcast(I32), rows.unsqueeze(0).to_broadcast([8, 4, T // 4]))
+        nc.sync.dma_start(words[:], x_words[0].rearrange("p t r -> p (t r)").bitcast(I32))
+        nc.sync.dma_start(w_raw[:], w1.rearrange("(p j) n -> p j n", j=PACK))
+        nc.sync.dma_start(zp_all[:], zp)
         nc.gpsimd.dma_start(csum_col[:], csum)
         nc.gpsimd.tensor_scalar(csum_neg[:], csum_col[:], -1.0, 0.0, ALU.mult, ALU.add)
 
@@ -48,7 +48,7 @@ def tile_picked_zeropt_none_p_kernel(tc, x_words, x_scales, zp, csum, w1, offs, 
         x_codes = pool.tile([P, S], U32, name="x_codes", align_bytes=64)
         nc.vector.tensor_copy(x_codes[:], words[:].bitcast(U32).indirect(offsets[:]))
 
-        w_grouped = pool.tile([P, N, PACK], BF16, name="w_grouped", align_bytes=64)
+        w_grouped = pool.tile([P, N, PACK], BF16, name="w_grouped", tag="w_grouped", align_bytes=64)
         nc.scalar.copy(w_grouped[:], w_raw[:].rearrange("p j n -> p n j"))
         w_codes = pool.tile([P, N], U32, name="w_codes", align_bytes=64)
         w_plane = pool.tile([P, N], U8, name="w_plane", align_bytes=64)
@@ -60,7 +60,7 @@ def tile_picked_zeropt_none_p_kernel(tc, x_words, x_scales, zp, csum, w1, offs, 
 
         picked = []
         for h in range(2):
-            zg = pool.tile([P, HALF], F32, name=f"zg{h}", align_bytes=64)
+            zg = pool.tile([P, HALF], F32, name=f"zg{h}", tag=("w_grouped", "zg1")[h], align_bytes=64)
             nc.vector.tensor_copy(zg[:], zp_all[:].indirect(offsets[:, h * HALF // 16 : (h + 1) * HALF // 16]))
             picked.append(zg)
         for h in range(2):

@@ -1,6 +1,7 @@
 from contextlib import ExitStack
 
 import concourse.mybir as mybir
+from concourse.masks import make_identity
 
 K, T, S, N = 512, 1024, 512, 128
 FLOPS = 2 * K * S * N
@@ -29,42 +30,51 @@ def tile_picked_zeropt_none_p_kernel(tc, x_words, x_scales, zp, csum, w1, offs, 
         words = pool.tile([P, T], I32, name="words", align_bytes=64)
         planes = pool.tile([P, T], U8, name="planes", align_bytes=64)
         zp_all = pool.tile([P, T], F32, name="zp_all", align_bytes=64)
-        w_raw = pool.tile([P, PACK, N], F32, name="w_raw", align_bytes=64)
+        w_raw = pool.tile([P, PACK, N], F32, name="w_raw", tag="w_raw", align_bytes=64)
         csum_col = pool.tile([P, 1], F32, name="csum_col")
-        csum_neg = pool.tile([P, 1], F32, name="csum_neg")
+        zp_row = pool.tile([P, T // P], F32, name="zp_row")
+        ident = pool.tile([P, P], F32, name="ident", tag="ident", align_bytes=64)
+        make_identity(nc, ident[:])
 
+        nc.sync.dma_start(zp_row[:], zp[0].rearrange("(p c) -> p c", p=P))
         nc.sync.dma_start(offsets[:], offs)
         for q in range(4):
             rows = x_scales[0, 4 * q : 4 * q + 4, :].bitcast(I32)
             (nc.scalar, nc.sync)[q // 2].dma_start(planes[32 * q : 32 * q + 32, :].bitcast(I32), rows.unsqueeze(0).to_broadcast([8, 4, T // 4]))
         nc.sync.dma_start(words[:], x_words[0].rearrange("p t r -> p (t r)").bitcast(I32))
         nc.sync.dma_start(w_raw[:], w1.rearrange("(p j) n -> p j n", j=PACK))
-        nc.sync.dma_start(zp_all[:], zp)
-        nc.gpsimd.dma_start(csum_col[:], csum)
-        nc.gpsimd.tensor_scalar(csum_neg[:], csum_col[:], -1.0, 0.0, ALU.mult, ALU.add)
+        nc.sync.dma_start(csum_col[:], csum)
+
+        zp_view = zp_all[:].rearrange("p (n c) -> p n c", c=T // P)
+        for b in range(2):
+            spread = psum.tile([P, 4, P], F32, name=f"spread{b}", tag=f"bank{b}")
+            for m in range(4):
+                col = 4 * b + m
+                nc.tensor.transpose(spread[:, m, :], zp_row[:, col : col + 1].to_broadcast([P, P]), ident[:])
+            nc.scalar.activation(zp_view[:, :, 4 * b : 4 * b + 4], spread[:].rearrange("p m n -> p n m"),
+                                 mybir.ActivationFunctionType.Copy, scale=-1.0)
 
         x_plane = pool.tile([P, S], U8, name="x_plane", align_bytes=64)
         nc.vector.tensor_copy(x_plane[:], planes[:].indirect(offsets[:]))
         x_codes = pool.tile([P, S], U32, name="x_codes", align_bytes=64)
         nc.vector.tensor_copy(x_codes[:], words[:].bitcast(U32).indirect(offsets[:]))
 
-        w_grouped = pool.tile([P, N, PACK], BF16, name="w_grouped", tag="w_grouped", align_bytes=64)
+        w_grouped = pool.tile([P, N, PACK], BF16, name="w_grouped", tag="ident", align_bytes=64)
         nc.scalar.copy(w_grouped[:], w_raw[:].rearrange("p j n -> p n j"))
         w_codes = pool.tile([P, N], U32, name="w_codes", align_bytes=64)
         w_plane = pool.tile([P, N], U8, name="w_plane", align_bytes=64)
         nc.vector.quantize_mx(out=w_codes[:].bitcast(FP8X4), scales=w_plane[:], in_=w_grouped[:].rearrange("p n j -> p (n j)"))
 
-        acc = psum.tile([N, S], F32, name="acc")
+
+        acc = psum.tile([N, S], F32, name="acc", tag="bank1")
         nc.tensor.matmul_mx(out=acc[:], lhsT=w_codes[:].bitcast(FP8X4), lhsT_scale=w_plane[:],
                             rhs=x_codes[:].bitcast(FP8X4), rhs_scale=x_plane[:], start=True, stop=True)
 
-        picked = []
+        zg = pool.tile([P, S], F32, name="zg", tag="w_raw", align_bytes=64)
         for h in range(2):
-            zg = pool.tile([P, HALF], F32, name=f"zg{h}", tag=("w_grouped", "zg1")[h], align_bytes=64)
-            nc.vector.tensor_copy(zg[:], zp_all[:].indirect(offsets[:, h * HALF // 16 : (h + 1) * HALF // 16]))
-            picked.append(zg)
+            nc.vector.tensor_copy(zg[:, h * HALF : (h + 1) * HALF], zp_all[:].indirect(offsets[:, h * HALF // 16 : (h + 1) * HALF // 16]))
         for h in range(2):
             cols = slice(h * HALF, (h + 1) * HALF)
             res = pool.tile([P, HALF], F32, name=f"res{h}", align_bytes=64)
-            nc.vector.scalar_tensor_tensor(res[:], picked[h][:], csum_neg[:], acc[:, cols], ALU.mult, ALU.add)
+            nc.vector.scalar_tensor_tensor(res[:], zg[:, cols], csum_col[:], acc[:, cols], ALU.mult, ALU.add)
             (nc.sync, nc.scalar)[h].dma_start(out[:, cols], res[:])

@@ -60,7 +60,7 @@ def tile_picked_zeropt_none_p_kernel(tc, x_words, x_scales, zp, csum, w1, offs, 
         nc.vector.tensor_copy(x_codes[:], words[:].bitcast(U32).indirect(offsets[:]))
 
         w_grouped = pool.tile([P, N, PACK], BF16, name="w_grouped", tag="ident", align_bytes=64)
-        nc.scalar.copy(w_grouped[:], w_raw[:].rearrange("p j n -> p n j"))
+        nc.scalar.copy(w_grouped[:].rearrange("p (c i) j -> p c j i", i=4), w_raw[:].rearrange("p j (c i) -> p c j i", i=4))
         w_codes = pool.tile([P, N], U32, name="w_codes", align_bytes=64)
         w_plane = pool.tile([P, N], U8, name="w_plane", align_bytes=64)
         nc.vector.quantize_mx(out=w_codes[:].bitcast(FP8X4), scales=w_plane[:], in_=w_grouped[:].rearrange("p n j -> p (n j)"))
@@ -77,4 +77,4 @@ def tile_picked_zeropt_none_p_kernel(tc, x_words, x_scales, zp, csum, w1, offs, 
             cols = slice(h * HALF, (h + 1) * HALF)
             res = pool.tile([P, HALF], F32, name=f"res{h}", align_bytes=64)
             nc.vector.scalar_tensor_tensor(res[:], zg[:, cols], csum_col[:], acc[:, cols], ALU.mult, ALU.add)
-            (nc.sync, nc.scalar)[h].dma_start(out[:, cols], res[:])
+            nc.sync.dma_start(out[:, cols], res[:])

@@ -17,64 +17,72 @@ ALU = mybir.AluOpType
 
 P = 128
 PACK = 4
-HALF = S // 2
+PIECE = 128
+PIECES = S // PIECE
 
 
 def tile_picked_zeropt_none_p_kernel(tc, x_words, x_scales, zp, csum, w1, offs, out):
     nc = tc.nc
     with ExitStack() as ctx:
         pool = ctx.enter_context(tc.tile_pool(name="held", bufs=1))
+        shared = ctx.enter_context(tc.tile_pool(name="shared", bufs=1))
         psum = ctx.enter_context(tc.psum_pool(name="psum", bufs=1))
 
         offsets = pool.tile([P, S // 16], U16, name="offsets")
         words = pool.tile([P, T], I32, name="words", align_bytes=64)
         planes = pool.tile([P, T], U8, name="planes", align_bytes=64)
         zp_all = pool.tile([P, T], F32, name="zp_all", align_bytes=64)
-        w_raw = pool.tile([P, PACK, N], F32, name="w_raw", tag="w_raw", align_bytes=64)
+        w_raw = shared.tile([P, PACK, N], F32, name="w_raw", offset=0, align_bytes=64)
         csum_col = pool.tile([P, 1], F32, name="csum_col")
         zp_row = pool.tile([P, T // P], F32, name="zp_row")
-        ident = pool.tile([P, P], F32, name="ident", tag="ident", align_bytes=64)
+        nc.gpsimd.dma_start(csum_col[:], csum)
+        ident = shared.tile([P, P], F32, name="ident", offset=4 * PACK * N, align_bytes=64)
         make_identity(nc, ident[:])
 
-        nc.sync.dma_start(zp_row[:], zp[0].rearrange("(p c) -> p c", p=P))
+        nc.vector.memset(planes[:].bitcast(I32), 0)
+
         nc.sync.dma_start(offsets[:], offs)
-        for q in range(4):
-            rows = x_scales[0, 4 * q : 4 * q + 4, :].bitcast(I32)
-            (nc.scalar, nc.sync)[q // 2].dma_start(planes[32 * q : 32 * q + 32, :].bitcast(I32), rows.unsqueeze(0).to_broadcast([8, 4, T // 4]))
-        nc.sync.dma_start(words[:], x_words[0].rearrange("p t r -> p (t r)").bitcast(I32))
+        nc.sync.dma_start(zp_row[:], zp[0].rearrange("(p c) -> p c", p=P))
         nc.sync.dma_start(w_raw[:], w1.rearrange("(p j) n -> p j n", j=PACK))
-        nc.sync.dma_start(csum_col[:], csum)
+        for q in range(4):
+            nc.sync.dma_start(planes[32 * q : 32 * q + 4, :].bitcast(I32), x_scales[0, 4 * q : 4 * q + 4, :].bitcast(I32))
+        nc.sync.dma_start(words[:], x_words[0].rearrange("p t r -> p (t r)").bitcast(I32))
+
+        minus_zp = pool.tile([P, T // P], F32, name="minus_zp")
+        nc.vector.tensor_scalar(minus_zp[:], zp_row[:], -1.0, None, ALU.mult)
+
+        w_grouped = pool.tile([P, N, PACK], BF16, name="w_grouped", align_bytes=64)
+        nc.scalar.copy(w_grouped[:].rearrange("p (c i) j -> p c j i", i=4), w_raw[:].rearrange("p j (c i) -> p c j i", i=4))
 
         zp_view = zp_all[:].rearrange("p (n c) -> p n c", c=T // P)
         for b in range(2):
             spread = psum.tile([P, 4, P], F32, name=f"spread{b}", tag=f"bank{b}")
             for m in range(4):
                 col = 4 * b + m
-                nc.tensor.transpose(spread[:, m, :], zp_row[:, col : col + 1].to_broadcast([P, P]), ident[:])
+                nc.tensor.transpose(spread[:, m, :], minus_zp[:, col : col + 1].to_broadcast([P, P]), ident[:])
             nc.scalar.activation(zp_view[:, :, 4 * b : 4 * b + 4], spread[:].rearrange("p m n -> p n m"),
-                                 mybir.ActivationFunctionType.Copy, scale=-1.0)
+                                 mybir.ActivationFunctionType.Copy, scale=csum_col[:])
 
         x_plane = pool.tile([P, S], U8, name="x_plane", align_bytes=64)
         nc.vector.tensor_copy(x_plane[:], planes[:].indirect(offsets[:]))
-        x_codes = pool.tile([P, S], U32, name="x_codes", align_bytes=64)
-        nc.vector.tensor_copy(x_codes[:], words[:].bitcast(U32).indirect(offsets[:]))
 
-        w_grouped = pool.tile([P, N, PACK], BF16, name="w_grouped", tag="ident", align_bytes=64)
-        nc.scalar.copy(w_grouped[:].rearrange("p (c i) j -> p c j i", i=4), w_raw[:].rearrange("p j (c i) -> p c j i", i=4))
         w_codes = pool.tile([P, N], U32, name="w_codes", align_bytes=64)
         w_plane = pool.tile([P, N], U8, name="w_plane", align_bytes=64)
         nc.vector.quantize_mx(out=w_codes[:].bitcast(FP8X4), scales=w_plane[:], in_=w_grouped[:].rearrange("p n j -> p (n j)"))
 
-
-        acc = psum.tile([N, S], F32, name="acc", tag="bank1")
-        nc.tensor.matmul_mx(out=acc[:], lhsT=w_codes[:].bitcast(FP8X4), lhsT_scale=w_plane[:],
-                            rhs=x_codes[:].bitcast(FP8X4), rhs_scale=x_plane[:], start=True, stop=True)
-
-        zg = pool.tile([P, S], F32, name="zg", tag="w_raw", align_bytes=64)
-        for h in range(2):
-            nc.vector.tensor_copy(zg[:, h * HALF : (h + 1) * HALF], zp_all[:].indirect(offsets[:, h * HALF // 16 : (h + 1) * HALF // 16]))
-        for h in range(2):
-            cols = slice(h * HALF, (h + 1) * HALF)
-            res = pool.tile([P, HALF], F32, name=f"res{h}", align_bytes=64)
-            nc.vector.scalar_tensor_tensor(res[:], zg[:, cols], csum_col[:], acc[:, cols], ALU.mult, ALU.add)
-            nc.sync.dma_start(out[:, cols], res[:])
+        x_codes = shared.tile([P, S], U32, name="x_codes", offset=4 * P, align_bytes=64)
+        y = pool.tile([P, S], F32, name="y", align_bytes=64)
+        res = pool.tile([P, S], F32, name="res", align_bytes=64)
+        for h in range(PIECES):
+            cols = slice(h * PIECE, (h + 1) * PIECE)
+            nc.vector.tensor_copy(x_codes[:, cols], words[:].bitcast(U32).indirect(offsets[:, h * PIECE // 16 : (h + 1) * PIECE // 16]))
+            acc = psum.tile([N, PIECE], F32, name=f"acc{h}", tag=f"bank{2 + h}")
+            nc.tensor.matmul_mx(out=acc[:], lhsT=w_codes[:].bitcast(FP8X4), lhsT_scale=w_plane[:],
+                                rhs=x_codes[:, cols].bitcast(FP8X4), rhs_scale=x_plane[:, cols], start=True, stop=True)
+            nc.scalar.copy(y[:, cols], acc[:])
+        for h in range(PIECES):
+            cols = slice(h * PIECE, (h + 1) * PIECE)
+            nc.vector.tensor_tensor(res[:, cols], zp_all[:].indirect(offsets[:, h * PIECE // 16 : (h + 1) * PIECE // 16]), y[:, cols], ALU.add)
+            if h % 2 == 1:
+                pair = slice((h - 1) * PIECE, (h + 1) * PIECE)
+                nc.sync.dma_start(out[:, pair], res[:, pair])

@@ -71,18 +71,22 @@ def tile_picked_zeropt_none_p_kernel(tc, x_words, x_scales, zp, csum, w1, offs, 
         nc.vector.quantize_mx(out=w_codes[:].bitcast(FP8X4), scales=w_plane[:], in_=w_grouped[:].rearrange("p n j -> p (n j)"))
 
         x_codes = shared.tile([P, S], U32, name="x_codes", offset=4 * P, align_bytes=64)
-        y = pool.tile([P, S], F32, name="y", align_bytes=64)
+        y = pool.tile([P, S - PIECE], F32, name="y", align_bytes=64)
         res = pool.tile([P, S], F32, name="res", align_bytes=64)
+        lists = [offsets[:, h * PIECE // 16 : (h + 1) * PIECE // 16] for h in range(PIECES)]
+        cols = [slice(h * PIECE, (h + 1) * PIECE) for h in range(PIECES)]
         for h in range(PIECES):
-            cols = slice(h * PIECE, (h + 1) * PIECE)
-            nc.vector.tensor_copy(x_codes[:, cols], words[:].bitcast(U32).indirect(offsets[:, h * PIECE // 16 : (h + 1) * PIECE // 16]))
+            nc.vector.tensor_copy(x_codes[:, cols[h]], words[:].bitcast(U32).indirect(lists[h]))
             acc = psum.tile([N, PIECE], F32, name=f"acc{h}", tag=f"bank{2 + h}")
             nc.tensor.matmul_mx(out=acc[:], lhsT=w_codes[:].bitcast(FP8X4), lhsT_scale=w_plane[:],
-                                rhs=x_codes[:, cols].bitcast(FP8X4), rhs_scale=x_plane[:, cols], start=True, stop=True)
-            nc.scalar.copy(y[:, cols], acc[:])
-        for h in range(PIECES):
-            cols = slice(h * PIECE, (h + 1) * PIECE)
-            nc.vector.tensor_tensor(res[:, cols], zp_all[:].indirect(offsets[:, h * PIECE // 16 : (h + 1) * PIECE // 16]), y[:, cols], ALU.add)
-            if h % 2 == 1:
-                pair = slice((h - 1) * PIECE, (h + 1) * PIECE)
-                nc.sync.dma_start(out[:, pair], res[:, pair])
+                                rhs=x_codes[:, cols[h]].bitcast(FP8X4), rhs_scale=x_plane[:, cols[h]], start=True, stop=True)
+            if h < PIECES - 1:
+                nc.scalar.copy(y[:, cols[h]], acc[:])
+        zg = pool.tile([P, PIECE], F32, name="zg", align_bytes=64)
+        nc.vector.tensor_copy(zg[:], zp_all[:].indirect(lists[-1]))
+        for h in range(PIECES - 1):
+            nc.vector.tensor_tensor(res[:, cols[h]], zp_all[:].indirect(lists[h]), y[:, cols[h]], ALU.add)
+            if h == 1:
+                nc.sync.dma_start(out[:, : 2 * PIECE], res[:, : 2 * PIECE])
+        nc.vector.tensor_tensor(res[:, cols[-1]], zg[:], acc[:], ALU.add)
+        nc.sync.dma_start(out[:, 2 * PIECE :], res[:, 2 * PIECE :])

@@ -35,7 +35,6 @@ def tile_picked_zeropt_none_p_kernel(tc, x_words, x_scales, zp, csum, w1, offs, 
         w_raw = shared.tile([P, PACK, N], F32, name="w_raw", offset=0, align_bytes=64)
         csum_col = pool.tile([P, 1], F32, name="csum_col")
         zp_row = pool.tile([P, T // P], F32, name="zp_row")
-        nc.gpsimd.dma_start(csum_col[:], csum)
         ident = shared.tile([P, P], F32, name="ident", offset=4 * PACK * N, align_bytes=64)
         make_identity(nc, ident[:])
 
@@ -47,6 +46,7 @@ def tile_picked_zeropt_none_p_kernel(tc, x_words, x_scales, zp, csum, w1, offs, 
         for q in range(4):
             nc.sync.dma_start(planes[32 * q : 32 * q + 4, :].bitcast(I32), x_scales[0, 4 * q : 4 * q + 4, :].bitcast(I32))
         nc.sync.dma_start(words[:], x_words[0].rearrange("p t r -> p (t r)").bitcast(I32))
+        nc.sync.dma_start(csum_col[:], csum)
 
         minus_zp = pool.tile([P, T // P], F32, name="minus_zp")
         nc.vector.tensor_scalar(minus_zp[:], zp_row[:], -1.0, None, ALU.mult)

@@ -40,11 +40,11 @@ def tile_picked_zeropt_none_p_kernel(tc, x_words, x_scales, zp, csum, w1, offs, 
 
         nc.vector.memset(planes[:].bitcast(I32), 0)
 
-        nc.sync.dma_start(offsets[:], offs)
         nc.sync.dma_start(zp_row[:], zp[0].rearrange("(p c) -> p c", p=P))
         nc.sync.dma_start(w_raw[:], w1.rearrange("(p j) n -> p j n", j=PACK))
+        nc.sync.dma_start(offsets[:], offs)
         for q in range(4):
-            nc.sync.dma_start(planes[32 * q : 32 * q + 4, :].bitcast(I32), x_scales[0, 4 * q : 4 * q + 4, :].bitcast(I32))
+            (nc.scalar if q == 0 else nc.sync).dma_start(planes[32 * q : 32 * q + 4, :].bitcast(I32), x_scales[0, 4 * q : 4 * q + 4, :].bitcast(I32))
         nc.sync.dma_start(words[:], x_words[0].rearrange("p t r -> p (t r)").bitcast(I32))
         nc.sync.dma_start(csum_col[:], csum)
 

@@ -36,9 +36,8 @@ def tile_picked_zeropt_none_p_kernel(tc, x_words, x_scales, zp, csum, w1, offs, 
         csum_col = pool.tile([P, 1], F32, name="csum_col")
         zp_row = pool.tile([P, T // P], F32, name="zp_row")
         ident = shared.tile([P, P], F32, name="ident", offset=4 * PACK * N, align_bytes=64)
+        nc.gpsimd.memset(planes[:].bitcast(I32), 0)
         make_identity(nc, ident[:])
-
-        nc.vector.memset(planes[:].bitcast(I32), 0)
 
         nc.sync.dma_start(zp_row[:], zp[0].rearrange("(p c) -> p c", p=P))
         nc.sync.dma_start(w_raw[:], w1.rearrange("(p j) n -> p j n", j=PACK))

@@ -87,5 +87,6 @@ def tile_picked_zeropt_none_p_kernel(tc, x_words, x_scales, zp, csum, w1, offs, 
             nc.vector.tensor_tensor(res[:, cols[h]], zp_all[:].indirect(lists[h]), y[:, cols[h]], ALU.add)
             if h == 1:
                 nc.sync.dma_start(out[:, : 2 * PIECE], res[:, : 2 * PIECE])
+        nc.scalar.dma_start(out[:, cols[2]], res[:, cols[2]])
         nc.vector.tensor_tensor(res[:, cols[-1]], zg[:], acc[:], ALU.add)
-        nc.sync.dma_start(out[:, 2 * PIECE :], res[:, 2 * PIECE :])
+        nc.sync.dma_start(out[:, cols[3]], res[:, cols[3]])

@@ -87,6 +87,6 @@ def tile_picked_zeropt_none_p_kernel(tc, x_words, x_scales, zp, csum, w1, offs, 
             nc.vector.tensor_tensor(res[:, cols[h]], zp_all[:].indirect(lists[h]), y[:, cols[h]], ALU.add)
             if h == 1:
                 nc.sync.dma_start(out[:, : 2 * PIECE], res[:, : 2 * PIECE])
-        nc.scalar.dma_start(out[:, cols[2]], res[:, cols[2]])
+        nc.sync.dma_start(out[:, cols[2]], res[:, cols[2]])
         nc.vector.tensor_tensor(res[:, cols[-1]], zg[:], acc[:], ALU.add)
         nc.sync.dma_start(out[:, cols[3]], res[:, cols[3]])

@@ -14,11 +14,13 @@ U16 = mybir.dt.uint16
 U8 = mybir.dt.uint8
 FP8X4 = mybir.dt.float8_e4m3fn_x4
 ALU = mybir.AluOpType
+COPY = mybir.ActivationFunctionType.Copy
 
 P = 128
 PACK = 4
-PIECE = 128
-PIECES = S // PIECE
+LATE = 128
+EARLY = S - LATE
+WIDTHS = (256, 128, 128)
 
 
 def tile_picked_zeropt_none_p_kernel(tc, x_words, x_scales, zp, csum, w1, offs, out):
@@ -31,36 +33,41 @@ def tile_picked_zeropt_none_p_kernel(tc, x_words, x_scales, zp, csum, w1, offs, 
         offsets = pool.tile([P, S // 16], U16, name="offsets")
         words = pool.tile([P, T], I32, name="words", align_bytes=64)
         planes = pool.tile([P, T], U8, name="planes", align_bytes=64)
+        zp_one = pool.tile([P, T], F32, name="zp_one", align_bytes=64)
         zp_all = pool.tile([P, T], F32, name="zp_all", align_bytes=64)
         w_raw = shared.tile([P, PACK, N], F32, name="w_raw", offset=0, align_bytes=64)
         csum_col = pool.tile([P, 1], F32, name="csum_col")
-        zp_row = pool.tile([P, T // P], F32, name="zp_row")
-        ident = shared.tile([P, P], F32, name="ident", offset=4 * PACK * N, align_bytes=64)
+        ident = pool.tile([P, P], F32, name="ident", align_bytes=64)
+        nc.vector.memset(zp_one[: P - 1, :].bitcast(I32), 0)
         nc.gpsimd.memset(planes[:].bitcast(I32), 0)
         make_identity(nc, ident[:])
 
-        nc.sync.dma_start(zp_row[:], zp[0].rearrange("(p c) -> p c", p=P))
-        nc.sync.dma_start(w_raw[:], w1.rearrange("(p j) n -> p j n", j=PACK))
         nc.sync.dma_start(offsets[:], offs)
+        nc.scalar.dma_start(zp_one[P - 1 :, :], zp[0:1, :])
+        nc.sync.dma_start(w_raw[:], w1.rearrange("(p j) n -> p j n", j=PACK))
         for q in range(4):
-            (nc.scalar if q == 0 else nc.sync).dma_start(planes[32 * q : 32 * q + 4, :].bitcast(I32), x_scales[0, 4 * q : 4 * q + 4, :].bitcast(I32))
+            nc.sync.dma_start(planes[32 * q : 32 * q + 4, :].bitcast(I32), x_scales[0, 4 * q : 4 * q + 4, :].bitcast(I32))
         nc.sync.dma_start(words[:], x_words[0].rearrange("p t r -> p (t r)").bitcast(I32))
         nc.sync.dma_start(csum_col[:], csum)
-
-        minus_zp = pool.tile([P, T // P], F32, name="minus_zp")
-        nc.vector.tensor_scalar(minus_zp[:], zp_row[:], -1.0, None, ALU.mult)
+        nc.sync.dma_start(zp_all[:], zp)
 
         w_grouped = pool.tile([P, N, PACK], BF16, name="w_grouped", align_bytes=64)
         nc.scalar.copy(w_grouped[:].rearrange("p (c i) j -> p c j i", i=4), w_raw[:].rearrange("p j (c i) -> p c j i", i=4))
 
-        zp_view = zp_all[:].rearrange("p (n c) -> p n c", c=T // P)
-        for b in range(2):
-            spread = psum.tile([P, 4, P], F32, name=f"spread{b}", tag=f"bank{b}")
-            for m in range(4):
-                col = 4 * b + m
-                nc.tensor.transpose(spread[:, m, :], minus_zp[:, col : col + 1].to_broadcast([P, P]), ident[:])
-            nc.scalar.activation(zp_view[:, :, 4 * b : 4 * b + 4], spread[:].rearrange("p m n -> p n m"),
-                                 mybir.ActivationFunctionType.Copy, scale=csum_col[:])
+        zg = pool.tile([P, EARLY], F32, name="zg", align_bytes=64)
+        nc.vector.tensor_copy(zg[:], zp_one[:].indirect(offsets[:, : EARLY // 16]))
+        turned = psum.tile([P, EARLY // P, P], F32, name="turned", tag="bank0")
+        for m in range(EARLY // P):
+            nc.tensor.transpose(turned[:, m, :], zg[:, m * P : (m + 1) * P], ident[:])
+        zg_cols = pool.tile([P, EARLY // P], F32, name="zg_cols")
+        nc.scalar.copy(zg_cols[:], turned[:, :, P - 1])
+        spread = psum.tile([P, EARLY // P, P], F32, name="spread", tag="bank1")
+        for m in range(EARLY // P):
+            nc.tensor.transpose(spread[:, m, :], zg_cols[:, m : m + 1].to_broadcast([P, P]), ident[:])
+        minus_csum = pool.tile([P, 1], F32, name="minus_csum")
+        nc.scalar.mul(minus_csum[:], csum_col[:], -1.0)
+        corr = pool.tile([P, EARLY], F32, name="corr", align_bytes=64)
+        nc.scalar.activation(corr[:], spread[:].rearrange("p m n -> p (m n)"), COPY, scale=minus_csum[:])
 
         x_plane = pool.tile([P, S], U8, name="x_plane", align_bytes=64)
         nc.vector.tensor_copy(x_plane[:], planes[:].indirect(offsets[:]))
@@ -69,24 +76,19 @@ def tile_picked_zeropt_none_p_kernel(tc, x_words, x_scales, zp, csum, w1, offs, 
         w_plane = pool.tile([P, N], U8, name="w_plane", align_bytes=64)
         nc.vector.quantize_mx(out=w_codes[:].bitcast(FP8X4), scales=w_plane[:], in_=w_grouped[:].rearrange("p n j -> p (n j)"))
 
-        x_codes = shared.tile([P, S], U32, name="x_codes", offset=4 * P, align_bytes=64)
-        y = pool.tile([P, S - PIECE], F32, name="y", align_bytes=64)
+        x_codes = shared.tile([P, S], U32, name="x_codes", offset=0, align_bytes=64)
         res = pool.tile([P, S], F32, name="res", align_bytes=64)
-        lists = [offsets[:, h * PIECE // 16 : (h + 1) * PIECE // 16] for h in range(PIECES)]
-        cols = [slice(h * PIECE, (h + 1) * PIECE) for h in range(PIECES)]
-        for h in range(PIECES):
-            nc.vector.tensor_copy(x_codes[:, cols[h]], words[:].bitcast(U32).indirect(lists[h]))
-            acc = psum.tile([N, PIECE], F32, name=f"acc{h}", tag=f"bank{2 + h}")
-            nc.tensor.matmul_mx(out=acc[:], lhsT=w_codes[:].bitcast(FP8X4), lhsT_scale=w_plane[:],
-                                rhs=x_codes[:, cols[h]].bitcast(FP8X4), rhs_scale=x_plane[:, cols[h]], start=True, stop=True)
-            if h < PIECES - 1:
-                nc.scalar.copy(y[:, cols[h]], acc[:])
-        zg = pool.tile([P, PIECE], F32, name="zg", align_bytes=64)
-        nc.vector.tensor_copy(zg[:], zp_all[:].indirect(lists[-1]))
-        for h in range(PIECES - 1):
-            nc.vector.tensor_tensor(res[:, cols[h]], zp_all[:].indirect(lists[h]), y[:, cols[h]], ALU.add)
-            if h == 1:
-                nc.sync.dma_start(out[:, : 2 * PIECE], res[:, : 2 * PIECE])
-        nc.sync.dma_start(out[:, cols[2]], res[:, cols[2]])
-        nc.vector.tensor_tensor(res[:, cols[-1]], zg[:], acc[:], ALU.add)
-        nc.sync.dma_start(out[:, cols[3]], res[:, cols[3]])
+        acc_early = psum.tile([N, EARLY], F32, name="acc_early", tag="bank0")
+        acc_late = psum.tile([N, LATE], F32, name="acc_late", tag="bank1")
+        pieces = [slice(sum(WIDTHS[:h]), sum(WIDTHS[: h + 1])) for h in range(len(WIDTHS))]
+        for cols in pieces:
+            nc.vector.tensor_copy(x_codes[:, cols], words[:].bitcast(U32).indirect(offsets[:, cols.start // 16 : cols.stop // 16]))
+            nc.tensor.matmul_mx(out=acc_late[:] if cols.stop == S else acc_early[:, cols], lhsT=w_codes[:].bitcast(FP8X4), lhsT_scale=w_plane[:],
+                                rhs=x_codes[:, cols].bitcast(FP8X4), rhs_scale=x_plane[:, cols], start=True, stop=True)
+        zg_late = pool.tile([P, LATE], F32, name="zg_late", align_bytes=64)
+        nc.vector.tensor_copy(zg_late[:], zp_all[:].indirect(offsets[:, EARLY // 16 :]))
+        for cols in pieces[:-1]:
+            nc.vector.tensor_tensor(res[:, cols], acc_early[:, cols], corr[:, cols], ALU.add)
+            nc.sync.dma_start(out[:, cols], res[:, cols])
+        nc.vector.scalar_tensor_tensor(res[:, EARLY:], zg_late[:], minus_csum[:], acc_late[:], ALU.mult, ALU.add)
+        nc.sync.dma_start(out[:, EARLY:], res[:, EARLY:])

@@ -54,20 +54,28 @@ def tile_picked_zeropt_none_p_kernel(tc, x_words, x_scales, zp, csum, w1, offs, 
         w_grouped = pool.tile([P, N, PACK], BF16, name="w_grouped", align_bytes=64)
         nc.scalar.copy(w_grouped[:].rearrange("p (c i) j -> p c j i", i=4), w_raw[:].rearrange("p j (c i) -> p c j i", i=4))
 
-        zg = pool.tile([P, EARLY], F32, name="zg", align_bytes=64)
-        nc.vector.tensor_copy(zg[:], zp_one[:].indirect(offsets[:, : EARLY // 16]))
-        turned = psum.tile([P, EARLY // P, P], F32, name="turned", tag="bank0")
-        for m in range(EARLY // P):
-            nc.tensor.transpose(turned[:, m, :], zg[:, m * P : (m + 1) * P], ident[:])
-        zg_cols = pool.tile([P, EARLY // P], F32, name="zg_cols")
-        nc.scalar.copy(zg_cols[:], turned[:, :, P - 1])
-        spread = psum.tile([P, EARLY // P, P], F32, name="spread", tag="bank1")
-        for m in range(EARLY // P):
-            nc.tensor.transpose(spread[:, m, :], zg_cols[:, m : m + 1].to_broadcast([P, P]), ident[:])
         minus_csum = pool.tile([P, 1], F32, name="minus_csum")
-        nc.scalar.mul(minus_csum[:], csum_col[:], -1.0)
+        nc.gpsimd.tensor_scalar(minus_csum[:], csum_col[:], -1.0, None, ALU.mult)
+        pieces = [slice(sum(WIDTHS[:h]), sum(WIDTHS[: h + 1])) for h in range(len(WIDTHS))]
+        zg = pool.tile([P, EARLY], F32, name="zg", align_bytes=64)
+        zg_cols = []
+        for h, cols in enumerate(pieces[:-1]):
+            nc.vector.tensor_copy(zg[:, cols], zp_one[:].indirect(offsets[:, cols.start // 16 : cols.stop // 16]))
+            turned = psum.tile([P, WIDTHS[h] // P, P], F32, name=f"turned{h}", tag=f"bank{h}")
+            for m in range(WIDTHS[h] // P):
+                nc.tensor.transpose(turned[:, m, :], zg[:, cols.start + m * P : cols.start + (m + 1) * P], ident[:])
+            col = pool.tile([P, WIDTHS[h] // P], F32, name=f"zg_cols{h}")
+            nc.scalar.copy(col[:], turned[:, :, P - 1])
+            zg_cols.append(col)
+        spreads = []
+        for h in range(len(WIDTHS) - 1):
+            spread = psum.tile([P, WIDTHS[h] // P, P], F32, name=f"spread{h}", tag=f"bank{2 + h}")
+            for m in range(WIDTHS[h] // P):
+                nc.tensor.transpose(spread[:, m, :], zg_cols[h][:, m : m + 1].to_broadcast([P, P]), ident[:])
+            spreads.append(spread)
         corr = pool.tile([P, EARLY], F32, name="corr", align_bytes=64)
-        nc.scalar.activation(corr[:], spread[:].rearrange("p m n -> p (m n)"), COPY, scale=minus_csum[:])
+        for h, cols in enumerate(pieces[:-1]):
+            nc.scalar.activation(corr[:, cols], spreads[h][:].rearrange("p m n -> p (m n)"), COPY, scale=minus_csum[:])
 
         x_plane = pool.tile([P, S], U8, name="x_plane", align_bytes=64)
         nc.vector.tensor_copy(x_plane[:], planes[:].indirect(offsets[:]))
@@ -78,17 +86,15 @@ def tile_picked_zeropt_none_p_kernel(tc, x_words, x_scales, zp, csum, w1, offs, 
 
         x_codes = shared.tile([P, S], U32, name="x_codes", offset=0, align_bytes=64)
         res = pool.tile([P, S], F32, name="res", align_bytes=64)
-        acc_early = psum.tile([N, EARLY], F32, name="acc_early", tag="bank0")
-        acc_late = psum.tile([N, LATE], F32, name="acc_late", tag="bank1")
-        pieces = [slice(sum(WIDTHS[:h]), sum(WIDTHS[: h + 1])) for h in range(len(WIDTHS))]
-        for cols in pieces:
+        accs = [psum.tile([N, WIDTHS[h]], F32, name=f"acc{h}", tag=f"bank{1 + h}") for h in range(len(WIDTHS))]
+        for cols, acc in zip(pieces, accs):
             nc.vector.tensor_copy(x_codes[:, cols], words[:].bitcast(U32).indirect(offsets[:, cols.start // 16 : cols.stop // 16]))
-            nc.tensor.matmul_mx(out=acc_late[:] if cols.stop == S else acc_early[:, cols], lhsT=w_codes[:].bitcast(FP8X4), lhsT_scale=w_plane[:],
+            nc.tensor.matmul_mx(out=acc[:], lhsT=w_codes[:].bitcast(FP8X4), lhsT_scale=w_plane[:],
                                 rhs=x_codes[:, cols].bitcast(FP8X4), rhs_scale=x_plane[:, cols], start=True, stop=True)
         zg_late = pool.tile([P, LATE], F32, name="zg_late", align_bytes=64)
         nc.vector.tensor_copy(zg_late[:], zp_all[:].indirect(offsets[:, EARLY // 16 :]))
-        for cols in pieces[:-1]:
-            nc.vector.tensor_tensor(res[:, cols], acc_early[:, cols], corr[:, cols], ALU.add)
+        for cols, acc in zip(pieces[:-1], accs):
+            nc.vector.tensor_tensor(res[:, cols], acc[:], corr[:, cols], ALU.add)
             nc.sync.dma_start(out[:, cols], res[:, cols])
-        nc.vector.scalar_tensor_tensor(res[:, EARLY:], zg_late[:], minus_csum[:], acc_late[:], ALU.mult, ALU.add)
+        nc.vector.scalar_tensor_tensor(res[:, EARLY:], zg_late[:], minus_csum[:], accs[-1][:], ALU.mult, ALU.add)
         nc.sync.dma_start(out[:, EARLY:], res[:, EARLY:])

@@ -18,9 +18,9 @@ COPY = mybir.ActivationFunctionType.Copy
 
 P = 128
 PACK = 4
-LATE = 128
+LATE = 256
 EARLY = S - LATE
-WIDTHS = (256, 128, 128)
+LAST = 128
 
 
 def tile_picked_zeropt_none_p_kernel(tc, x_words, x_scales, zp, csum, w1, offs, out):
@@ -54,28 +54,20 @@ def tile_picked_zeropt_none_p_kernel(tc, x_words, x_scales, zp, csum, w1, offs, 
         w_grouped = pool.tile([P, N, PACK], BF16, name="w_grouped", align_bytes=64)
         nc.scalar.copy(w_grouped[:].rearrange("p (c i) j -> p c j i", i=4), w_raw[:].rearrange("p j (c i) -> p c j i", i=4))
 
+        zg = pool.tile([P, EARLY], F32, name="zg", align_bytes=64)
+        nc.vector.tensor_copy(zg[:], zp_one[:].indirect(offsets[:, : EARLY // 16]))
+        turned = psum.tile([P, EARLY // P, P], F32, name="turned", tag="bank0")
+        for m in range(EARLY // P):
+            nc.tensor.transpose(turned[:, m, :], zg[:, m * P : (m + 1) * P], ident[:])
+        zg_cols = pool.tile([P, EARLY // P], F32, name="zg_cols")
+        nc.scalar.copy(zg_cols[:], turned[:, :, P - 1])
+        spread = psum.tile([P, EARLY // P, P], F32, name="spread", tag="bank1")
+        for m in range(EARLY // P):
+            nc.tensor.transpose(spread[:, m, :], zg_cols[:, m : m + 1].to_broadcast([P, P]), ident[:])
         minus_csum = pool.tile([P, 1], F32, name="minus_csum")
         nc.gpsimd.tensor_scalar(minus_csum[:], csum_col[:], -1.0, None, ALU.mult)
-        pieces = [slice(sum(WIDTHS[:h]), sum(WIDTHS[: h + 1])) for h in range(len(WIDTHS))]
-        zg = pool.tile([P, EARLY], F32, name="zg", align_bytes=64)
-        zg_cols = []
-        for h, cols in enumerate(pieces[:-1]):
-            nc.vector.tensor_copy(zg[:, cols], zp_one[:].indirect(offsets[:, cols.start // 16 : cols.stop // 16]))
-            turned = psum.tile([P, WIDTHS[h] // P, P], F32, name=f"turned{h}", tag=f"bank{h}")
-            for m in range(WIDTHS[h] // P):
-                nc.tensor.transpose(turned[:, m, :], zg[:, cols.start + m * P : cols.start + (m + 1) * P], ident[:])
-            col = pool.tile([P, WIDTHS[h] // P], F32, name=f"zg_cols{h}")
-            nc.scalar.copy(col[:], turned[:, :, P - 1])
-            zg_cols.append(col)
-        spreads = []
-        for h in range(len(WIDTHS) - 1):
-            spread = psum.tile([P, WIDTHS[h] // P, P], F32, name=f"spread{h}", tag=f"bank{2 + h}")
-            for m in range(WIDTHS[h] // P):
-                nc.tensor.transpose(spread[:, m, :], zg_cols[h][:, m : m + 1].to_broadcast([P, P]), ident[:])
-            spreads.append(spread)
         corr = pool.tile([P, EARLY], F32, name="corr", align_bytes=64)
-        for h, cols in enumerate(pieces[:-1]):
-            nc.scalar.activation(corr[:, cols], spreads[h][:].rearrange("p m n -> p (m n)"), COPY, scale=minus_csum[:])
+        nc.scalar.activation(corr[:], spread[:].rearrange("p m n -> p (m n)"), COPY, scale=minus_csum[:])
 
         x_plane = pool.tile([P, S], U8, name="x_plane", align_bytes=64)
         nc.vector.tensor_copy(x_plane[:], planes[:].indirect(offsets[:]))
@@ -86,15 +78,16 @@ def tile_picked_zeropt_none_p_kernel(tc, x_words, x_scales, zp, csum, w1, offs, 
 
         x_codes = shared.tile([P, S], U32, name="x_codes", offset=0, align_bytes=64)
         res = pool.tile([P, S], F32, name="res", align_bytes=64)
-        accs = [psum.tile([N, WIDTHS[h]], F32, name=f"acc{h}", tag=f"bank{1 + h}") for h in range(len(WIDTHS))]
-        for cols, acc in zip(pieces, accs):
+        acc_early = psum.tile([N, EARLY], F32, name="acc_early", tag="bank0")
+        acc_late = psum.tile([N, LATE], F32, name="acc_late", tag="bank1")
+        for cols, acc in ((slice(0, EARLY), acc_early), (slice(EARLY, S), acc_late)):
             nc.vector.tensor_copy(x_codes[:, cols], words[:].bitcast(U32).indirect(offsets[:, cols.start // 16 : cols.stop // 16]))
             nc.tensor.matmul_mx(out=acc[:], lhsT=w_codes[:].bitcast(FP8X4), lhsT_scale=w_plane[:],
                                 rhs=x_codes[:, cols].bitcast(FP8X4), rhs_scale=x_plane[:, cols], start=True, stop=True)
         zg_late = pool.tile([P, LATE], F32, name="zg_late", align_bytes=64)
         nc.vector.tensor_copy(zg_late[:], zp_all[:].indirect(offsets[:, EARLY // 16 :]))
-        for cols, acc in zip(pieces[:-1], accs):
-            nc.vector.tensor_tensor(res[:, cols], acc[:], corr[:, cols], ALU.add)
-            nc.sync.dma_start(out[:, cols], res[:, cols])
-        nc.vector.scalar_tensor_tensor(res[:, EARLY:], zg_late[:], minus_csum[:], accs[-1][:], ALU.mult, ALU.add)
-        nc.sync.dma_start(out[:, EARLY:], res[:, EARLY:])
+        nc.vector.tensor_tensor(res[:, :EARLY], acc_early[:], corr[:], ALU.add)
+        nc.sync.dma_start(out[:, :EARLY], res[:, :EARLY])
+        for lo, hi in ((0, LATE - LAST), (LATE - LAST, LATE)):
+            nc.vector.scalar_tensor_tensor(res[:, EARLY + lo : EARLY + hi], zg_late[:, lo:hi], minus_csum[:], acc_late[:, lo:hi], ALU.mult, ALU.add)
+            nc.sync.dma_start(out[:, EARLY + lo : EARLY + hi], res[:, EARLY + lo : EARLY + hi])

@@ -46,7 +46,7 @@ def tile_picked_zeropt_none_p_kernel(tc, x_words, x_scales, zp, csum, w1, offs, 
         nc.scalar.dma_start(zp_one[P - 1 :, :], zp[0:1, :])
         nc.sync.dma_start(w_raw[:], w1.rearrange("(p j) n -> p j n", j=PACK))
         for q in range(4):
-            nc.sync.dma_start(planes[32 * q : 32 * q + 4, :].bitcast(I32), x_scales[0, 4 * q : 4 * q + 4, :].bitcast(I32))
+            (nc.scalar if q == 0 else nc.sync).dma_start(planes[32 * q : 32 * q + 4, :].bitcast(I32), x_scales[0, 4 * q : 4 * q + 4, :].bitcast(I32))
         nc.sync.dma_start(words[:], x_words[0].rearrange("p t r -> p (t r)").bitcast(I32))
         nc.sync.dma_start(csum_col[:], csum)
         nc.sync.dma_start(zp_all[:], zp)

@@ -48,8 +48,8 @@ def tile_picked_zeropt_none_p_kernel(tc, x_words, x_scales, zp, csum, w1, offs, 
         for q in range(4):
             (nc.scalar if q == 0 else nc.sync).dma_start(planes[32 * q : 32 * q + 4, :].bitcast(I32), x_scales[0, 4 * q : 4 * q + 4, :].bitcast(I32))
         nc.sync.dma_start(words[:], x_words[0].rearrange("p t r -> p (t r)").bitcast(I32))
-        nc.sync.dma_start(csum_col[:], csum)
         nc.sync.dma_start(zp_all[:], zp)
+        nc.sync.dma_start(csum_col[:], csum)
 
         w_grouped = pool.tile([P, N, PACK], BF16, name="w_grouped", align_bytes=64)
         nc.scalar.copy(w_grouped[:].rearrange("p (c i) j -> p c j i", i=4), w_raw[:].rearrange("p j (c i) -> p c j i", i=4))
@@ -67,7 +67,7 @@ def tile_picked_zeropt_none_p_kernel(tc, x_words, x_scales, zp, csum, w1, offs, 
         minus_csum = pool.tile([P, 1], F32, name="minus_csum")
         nc.gpsimd.tensor_scalar(minus_csum[:], csum_col[:], -1.0, None, ALU.mult)
         corr = pool.tile([P, EARLY], F32, name="corr", align_bytes=64)
-        nc.scalar.activation(corr[:], spread[:].rearrange("p m n -> p (m n)"), COPY, scale=minus_csum[:])
+        nc.scalar.activation(corr[:], spread[:].rearrange("p m n -> p (m n)"), COPY)
 
         x_plane = pool.tile([P, S], U8, name="x_plane", align_bytes=64)
         nc.vector.tensor_copy(x_plane[:], planes[:].indirect(offsets[:]))
@@ -86,7 +86,7 @@ def tile_picked_zeropt_none_p_kernel(tc, x_words, x_scales, zp, csum, w1, offs, 
                                 rhs=x_codes[:, cols].bitcast(FP8X4), rhs_scale=x_plane[:, cols], start=True, stop=True)
         zg_late = pool.tile([P, LATE], F32, name="zg_late", align_bytes=64)
         nc.vector.tensor_copy(zg_late[:], zp_all[:].indirect(offsets[:, EARLY // 16 :]))
-        nc.vector.tensor_tensor(res[:, :EARLY], acc_early[:], corr[:], ALU.add)
+        nc.vector.scalar_tensor_tensor(res[:, :EARLY], corr[:], minus_csum[:], acc_early[:], ALU.mult, ALU.add)
         nc.sync.dma_start(out[:, :EARLY], res[:, :EARLY])
         for lo, hi in ((0, LATE - LAST), (LATE - LAST, LATE)):
             nc.vector.scalar_tensor_tensor(res[:, EARLY + lo : EARLY + hi], zg_late[:, lo:hi], minus_csum[:], acc_late[:, lo:hi], ALU.mult, ALU.add)

@@ -18,8 +18,8 @@ COPY = mybir.ActivationFunctionType.Copy
 
 P = 128
 PACK = 4
-LATE = 256
-EARLY = S - LATE
+HALF = S // 2
+EARLY = 288
 LAST = 128
 
 
@@ -56,18 +56,22 @@ def tile_picked_zeropt_none_p_kernel(tc, x_words, x_scales, zp, csum, w1, offs, 
 
         zg = pool.tile([P, EARLY], F32, name="zg", align_bytes=64)
         nc.vector.tensor_copy(zg[:], zp_one[:].indirect(offsets[:, : EARLY // 16]))
-        turned = psum.tile([P, EARLY // P, P], F32, name="turned", tag="bank0")
-        for m in range(EARLY // P):
-            nc.tensor.transpose(turned[:, m, :], zg[:, m * P : (m + 1) * P], ident[:])
-        zg_cols = pool.tile([P, EARLY // P], F32, name="zg_cols")
+        starts = [min(lo, EARLY - P) for lo in range(0, EARLY, P)]
+        turned = psum.tile([P, len(starts), P], F32, name="turned", tag="bank0")
+        for m, lo in enumerate(starts):
+            nc.tensor.transpose(turned[:, m, :], zg[:, lo : lo + P], ident[:])
+        zg_cols = pool.tile([P, len(starts)], F32, name="zg_cols")
         nc.scalar.copy(zg_cols[:], turned[:, :, P - 1])
-        spread = psum.tile([P, EARLY // P, P], F32, name="spread", tag="bank1")
-        for m in range(EARLY // P):
-            nc.tensor.transpose(spread[:, m, :], zg_cols[:, m : m + 1].to_broadcast([P, P]), ident[:])
+        spread_a = psum.tile([P, P], F32, name="spread_a", tag="bank1")
+        spread_b = psum.tile([P, EARLY - P], F32, name="spread_b", tag="bank2")
+        for m, lo in enumerate(starts):
+            target = spread_a[:] if m == 0 else spread_b[:, lo - P : lo]
+            nc.tensor.transpose(target, zg_cols[:, m : m + 1].to_broadcast([P, P]), ident[:])
         minus_csum = pool.tile([P, 1], F32, name="minus_csum")
         nc.gpsimd.tensor_scalar(minus_csum[:], csum_col[:], -1.0, None, ALU.mult)
-        corr = pool.tile([P, EARLY], F32, name="corr", align_bytes=64)
-        nc.scalar.activation(corr[:], spread[:].rearrange("p m n -> p (m n)"), COPY)
+        zg_all = pool.tile([P, S], F32, name="zg_all", align_bytes=64)
+        nc.scalar.activation(zg_all[:, :P], spread_a[:], COPY)
+        nc.scalar.activation(zg_all[:, P:EARLY], spread_b[:], COPY)
 
         x_plane = pool.tile([P, S], U8, name="x_plane", align_bytes=64)
         nc.vector.tensor_copy(x_plane[:], planes[:].indirect(offsets[:]))
@@ -78,16 +82,17 @@ def tile_picked_zeropt_none_p_kernel(tc, x_words, x_scales, zp, csum, w1, offs, 
 
         x_codes = shared.tile([P, S], U32, name="x_codes", offset=0, align_bytes=64)
         res = pool.tile([P, S], F32, name="res", align_bytes=64)
-        acc_early = psum.tile([N, EARLY], F32, name="acc_early", tag="bank0")
-        acc_late = psum.tile([N, LATE], F32, name="acc_late", tag="bank1")
-        for cols, acc in ((slice(0, EARLY), acc_early), (slice(EARLY, S), acc_late)):
-            nc.vector.tensor_copy(x_codes[:, cols], words[:].bitcast(U32).indirect(offsets[:, cols.start // 16 : cols.stop // 16]))
-            nc.tensor.matmul_mx(out=acc[:], lhsT=w_codes[:].bitcast(FP8X4), lhsT_scale=w_plane[:],
-                                rhs=x_codes[:, cols].bitcast(FP8X4), rhs_scale=x_plane[:, cols], start=True, stop=True)
-        zg_late = pool.tile([P, LATE], F32, name="zg_late", align_bytes=64)
-        nc.vector.tensor_copy(zg_late[:], zp_all[:].indirect(offsets[:, EARLY // 16 :]))
-        nc.vector.scalar_tensor_tensor(res[:, :EARLY], corr[:], minus_csum[:], acc_early[:], ALU.mult, ALU.add)
-        nc.sync.dma_start(out[:, :EARLY], res[:, :EARLY])
-        for lo, hi in ((0, LATE - LAST), (LATE - LAST, LATE)):
-            nc.vector.scalar_tensor_tensor(res[:, EARLY + lo : EARLY + hi], zg_late[:, lo:hi], minus_csum[:], acc_late[:, lo:hi], ALU.mult, ALU.add)
-            nc.sync.dma_start(out[:, EARLY + lo : EARLY + hi], res[:, EARLY + lo : EARLY + hi])
+        acc_first = psum.tile([N, HALF], F32, name="acc_first", tag="bank0")
+        acc_mid = psum.tile([N, HALF - LAST], F32, name="acc_mid", tag="bank1")
+        acc_last = psum.tile([N, LAST], F32, name="acc_last", tag="bank2")
+        pieces = ((0, HALF, acc_first), (HALF, S - LAST, acc_mid), (S - LAST, S, acc_last))
+        for group in (pieces[:1], pieces[1:]):
+            lo, hi = group[0][0], group[-1][1]
+            nc.vector.tensor_copy(x_codes[:, lo:hi], words[:].bitcast(U32).indirect(offsets[:, lo // 16 : hi // 16]))
+            for lo, hi, acc in group:
+                nc.tensor.matmul_mx(out=acc[:], lhsT=w_codes[:].bitcast(FP8X4), lhsT_scale=w_plane[:],
+                                    rhs=x_codes[:, lo:hi].bitcast(FP8X4), rhs_scale=x_plane[:, lo:hi], start=True, stop=True)
+        nc.vector.tensor_copy(zg_all[:, EARLY:], zp_all[:].indirect(offsets[:, EARLY // 16 :]))
+        for lo, hi, acc in pieces:
+            nc.vector.scalar_tensor_tensor(res[:, lo:hi], zg_all[:, lo:hi], minus_csum[:], acc[:], ALU.mult, ALU.add)
+            nc.sync.dma_start(out[:, lo:hi], res[:, lo:hi])

@@ -19,7 +19,7 @@ COPY = mybir.ActivationFunctionType.Copy
 P = 128
 PACK = 4
 HALF = S // 2
-EARLY = 288
+EARLY = 320
 LAST = 128
 
 

@@ -19,7 +19,7 @@ COPY = mybir.ActivationFunctionType.Copy
 P = 128
 PACK = 4
 HALF = S // 2
-EARLY = 320
+EARLY = 384
 LAST = 128
 
 
@@ -57,21 +57,21 @@ def tile_picked_zeropt_none_p_kernel(tc, x_words, x_scales, zp, csum, w1, offs, 
         zg = pool.tile([P, EARLY], F32, name="zg", align_bytes=64)
         nc.vector.tensor_copy(zg[:], zp_one[:].indirect(offsets[:, : EARLY // 16]))
         starts = [min(lo, EARLY - P) for lo in range(0, EARLY, P)]
-        turned = psum.tile([P, len(starts), P], F32, name="turned", tag="bank0")
+        turned = [psum.tile([P, P], F32, name=f"turned{m}", tag=f"turn{m}") for m in range(len(starts))]
         for m, lo in enumerate(starts):
-            nc.tensor.transpose(turned[:, m, :], zg[:, lo : lo + P], ident[:])
-        zg_cols = pool.tile([P, len(starts)], F32, name="zg_cols")
-        nc.scalar.copy(zg_cols[:], turned[:, :, P - 1])
-        spread_a = psum.tile([P, P], F32, name="spread_a", tag="bank1")
-        spread_b = psum.tile([P, EARLY - P], F32, name="spread_b", tag="bank2")
-        for m, lo in enumerate(starts):
-            target = spread_a[:] if m == 0 else spread_b[:, lo - P : lo]
-            nc.tensor.transpose(target, zg_cols[:, m : m + 1].to_broadcast([P, P]), ident[:])
+            nc.tensor.transpose(turned[m][:], zg[:, lo : lo + P], ident[:])
+        zg_cols = [pool.tile([P, 1], F32, name=f"zg_col{m}") for m in range(len(starts))]
+        for m in range(len(starts)):
+            nc.scalar.copy(zg_cols[m][:], turned[m][:, P - 1 :])
+        spread = [psum.tile([P, P], F32, name=f"spread{m}", tag=f"spread{m}") for m in range(len(starts))]
+        for m in range(len(starts)):
+            nc.tensor.transpose(spread[m][:], zg_cols[m][:].to_broadcast([P, P]), ident[:])
         minus_csum = pool.tile([P, 1], F32, name="minus_csum")
         nc.gpsimd.tensor_scalar(minus_csum[:], csum_col[:], -1.0, None, ALU.mult)
         zg_all = pool.tile([P, S], F32, name="zg_all", align_bytes=64)
-        nc.scalar.activation(zg_all[:, :P], spread_a[:], COPY)
-        nc.scalar.activation(zg_all[:, P:EARLY], spread_b[:], COPY)
+        for m, lo in enumerate(starts):
+            done = m * P
+            nc.scalar.activation(zg_all[:, done : lo + P], spread[m][:, done - lo :], COPY)
 
         x_plane = pool.tile([P, S], U8, name="x_plane", align_bytes=64)
         nc.vector.tensor_copy(x_plane[:], planes[:].indirect(offsets[:]))
@@ -82,11 +82,11 @@ def tile_picked_zeropt_none_p_kernel(tc, x_words, x_scales, zp, csum, w1, offs, 
 
         x_codes = shared.tile([P, S], U32, name="x_codes", offset=0, align_bytes=64)
         res = pool.tile([P, S], F32, name="res", align_bytes=64)
-        acc_first = psum.tile([N, HALF], F32, name="acc_first", tag="bank0")
-        acc_mid = psum.tile([N, HALF - LAST], F32, name="acc_mid", tag="bank1")
-        acc_last = psum.tile([N, LAST], F32, name="acc_last", tag="bank2")
+        acc_first = psum.tile([N, HALF], F32, name="acc_first", tag="turn2")
+        acc_mid = psum.tile([N, HALF - LAST], F32, name="acc_mid", tag="spread1")
+        acc_last = psum.tile([N, LAST], F32, name="acc_last", tag="spread2")
         pieces = ((0, HALF, acc_first), (HALF, S - LAST, acc_mid), (S - LAST, S, acc_last))
-        for group in (pieces[:1], pieces[1:]):
+        for group in (pieces[:1], pieces[1:2], pieces[2:]):
             lo, hi = group[0][0], group[-1][1]
             nc.vector.tensor_copy(x_codes[:, lo:hi], words[:].bitcast(U32).indirect(offsets[:, lo // 16 : hi // 16]))
             for lo, hi, acc in group:

@@ -30,14 +30,14 @@ def tile_picked_zeropt_none_p_kernel(tc, x_words, x_scales, zp, csum, w1, offs, 
         shared = ctx.enter_context(tc.tile_pool(name="shared", bufs=1))
         psum = ctx.enter_context(tc.psum_pool(name="psum", bufs=1))
 
-        offsets = pool.tile([P, S // 16], U16, name="offsets")
-        words = pool.tile([P, T], I32, name="words", align_bytes=64)
-        planes = pool.tile([P, T], U8, name="planes", align_bytes=64)
-        zp_one = pool.tile([P, T], F32, name="zp_one", align_bytes=64)
-        zp_all = pool.tile([P, T], F32, name="zp_all", align_bytes=64)
-        w_raw = shared.tile([P, PACK, N], F32, name="w_raw", offset=0, align_bytes=64)
+        offsets = pool.tile([P, S // 16], U16, name="offsets", align_bytes=256)
+        words = pool.tile([P, T], I32, name="words", align_bytes=256)
+        planes = pool.tile([P, T], U8, name="planes", align_bytes=256)
+        zp_one = pool.tile([P, T], F32, name="zp_one", align_bytes=256)
+        zp_all = pool.tile([P, T], F32, name="zp_all", align_bytes=256)
+        w_raw = shared.tile([P, PACK, N], F32, name="w_raw", offset=0, align_bytes=256)
         csum_col = pool.tile([P, 1], F32, name="csum_col")
-        ident = pool.tile([P, P], F32, name="ident", align_bytes=64)
+        ident = pool.tile([P, P], F32, name="ident", align_bytes=256)
         nc.vector.memset(zp_one[: P - 1, :].bitcast(I32), 0)
         nc.gpsimd.memset(planes[:].bitcast(I32), 0)
         make_identity(nc, ident[:])
@@ -51,10 +51,10 @@ def tile_picked_zeropt_none_p_kernel(tc, x_words, x_scales, zp, csum, w1, offs, 
         nc.sync.dma_start(zp_all[:], zp)
         nc.sync.dma_start(csum_col[:], csum)
 
-        w_grouped = pool.tile([P, N, PACK], BF16, name="w_grouped", align_bytes=64)
+        w_grouped = pool.tile([P, N, PACK], BF16, name="w_grouped", align_bytes=256)
         nc.scalar.copy(w_grouped[:].rearrange("p (c i) j -> p c j i", i=4), w_raw[:].rearrange("p j (c i) -> p c j i", i=4))
 
-        zg = pool.tile([P, EARLY], F32, name="zg", align_bytes=64)
+        zg = pool.tile([P, EARLY], F32, name="zg", align_bytes=256)
         nc.vector.tensor_copy(zg[:], zp_one[:].indirect(offsets[:, : EARLY // 16]))
         starts = [min(lo, EARLY - P) for lo in range(0, EARLY, P)]
         turned = [psum.tile([P, P], F32, name=f"turned{m}", tag=f"turn{m}") for m in range(len(starts))]
@@ -68,20 +68,20 @@ def tile_picked_zeropt_none_p_kernel(tc, x_words, x_scales, zp, csum, w1, offs, 
             nc.tensor.transpose(spread[m][:], zg_cols[m][:].to_broadcast([P, P]), ident[:])
         minus_csum = pool.tile([P, 1], F32, name="minus_csum")
         nc.gpsimd.tensor_scalar(minus_csum[:], csum_col[:], -1.0, None, ALU.mult)
-        zg_all = pool.tile([P, S], F32, name="zg_all", align_bytes=64)
+        zg_all = pool.tile([P, S], F32, name="zg_all", align_bytes=256)
         for m, lo in enumerate(starts):
             done = m * P
             nc.scalar.activation(zg_all[:, done : lo + P], spread[m][:, done - lo :], COPY)
 
-        x_plane = pool.tile([P, S], U8, name="x_plane", align_bytes=64)
+        x_plane = pool.tile([P, S], U8, name="x_plane", align_bytes=256)
         nc.vector.tensor_copy(x_plane[:], planes[:].indirect(offsets[:]))
 
-        w_codes = pool.tile([P, N], U32, name="w_codes", align_bytes=64)
-        w_plane = pool.tile([P, N], U8, name="w_plane", align_bytes=64)
+        w_codes = pool.tile([P, N], U32, name="w_codes", align_bytes=256)
+        w_plane = pool.tile([P, N], U8, name="w_plane", align_bytes=256)
         nc.vector.quantize_mx(out=w_codes[:].bitcast(FP8X4), scales=w_plane[:], in_=w_grouped[:].rearrange("p n j -> p (n j)"))
 
-        x_codes = shared.tile([P, S], U32, name="x_codes", offset=0, align_bytes=64)
-        res = pool.tile([P, S], F32, name="res", align_bytes=64)
+        x_codes = shared.tile([P, S], U32, name="x_codes", offset=0, align_bytes=256)
+        res = pool.tile([P, S], F32, name="res", align_bytes=256)
         acc_first = psum.tile([N, HALF], F32, name="acc_first", tag="turn2")
         acc_mid = psum.tile([N, HALF - LAST], F32, name="acc_mid", tag="spread1")
         acc_last = psum.tile([N, LAST], F32, name="acc_last", tag="spread2")

@@ -93,6 +93,11 @@ def tile_picked_zeropt_none_p_kernel(tc, x_words, x_scales, zp, csum, w1, offs, 
                 nc.tensor.matmul_mx(out=acc[:], lhsT=w_codes[:].bitcast(FP8X4), lhsT_scale=w_plane[:],
                                     rhs=x_codes[:, lo:hi].bitcast(FP8X4), rhs_scale=x_plane[:, lo:hi], start=True, stop=True)
         nc.vector.tensor_copy(zg_all[:, EARLY:], zp_all[:].indirect(offsets[:, EARLY // 16 :]))
-        for lo, hi, acc in pieces:
-            nc.vector.scalar_tensor_tensor(res[:, lo:hi], zg_all[:, lo:hi], minus_csum[:], acc[:], ALU.mult, ALU.add)
-            nc.sync.dma_start(out[:, lo:hi], res[:, lo:hi])
+        stored = 0
+        for first, last, acc in pieces:
+            for lo in range(first, last, P):
+                hi = lo + P
+                nc.vector.scalar_tensor_tensor(res[:, lo:hi], zg_all[:, lo:hi], minus_csum[:], acc[:, lo - first : hi - first], ALU.mult, ALU.add)
+                if hi <= HALF or hi == S:
+                    nc.sync.dma_start(out[:, stored:hi], res[:, stored:hi])
+                    stored = hi

@@ -48,7 +48,8 @@ def tile_picked_zeropt_none_p_kernel(tc, x_words, x_scales, zp, csum, w1, offs, 
         for q in range(4):
             (nc.scalar if q == 0 else nc.sync).dma_start(planes[32 * q : 32 * q + 4, :].bitcast(I32), x_scales[0, 4 * q : 4 * q + 4, :].bitcast(I32))
         nc.sync.dma_start(words[:], x_words[0].rearrange("p t r -> p (t r)").bitcast(I32))
-        nc.sync.dma_start(zp_all[:], zp)
+        for lo, hi in ((0, 384), (384, 768), (768, T)):
+            nc.sync.dma_start(zp_all[:, lo:hi], zp[:, lo:hi])
         nc.sync.dma_start(csum_col[:], csum)
 
         w_grouped = pool.tile([P, N, PACK], BF16, name="w_grouped", align_bytes=256)

@@ -20,7 +20,7 @@ P = 128
 PACK = 4
 HALF = S // 2
 EARLY = 384
-LAST = 128
+LATE = S - EARLY
 
 
 def tile_picked_zeropt_none_p_kernel(tc, x_words, x_scales, zp, csum, w1, offs, out):
@@ -28,6 +28,7 @@ def tile_picked_zeropt_none_p_kernel(tc, x_words, x_scales, zp, csum, w1, offs, 
     with ExitStack() as ctx:
         pool = ctx.enter_context(tc.tile_pool(name="held", bufs=1))
         shared = ctx.enter_context(tc.tile_pool(name="shared", bufs=1))
+        late = ctx.enter_context(tc.tile_pool(name="late", bufs=1))
         psum = ctx.enter_context(tc.psum_pool(name="psum", bufs=1))
 
         offsets = pool.tile([P, S // 16], U16, name="offsets", align_bytes=256)
@@ -48,20 +49,20 @@ def tile_picked_zeropt_none_p_kernel(tc, x_words, x_scales, zp, csum, w1, offs, 
         for q in range(4):
             (nc.scalar if q == 0 else nc.sync).dma_start(planes[32 * q : 32 * q + 4, :].bitcast(I32), x_scales[0, 4 * q : 4 * q + 4, :].bitcast(I32))
         nc.sync.dma_start(words[:], x_words[0].rearrange("p t r -> p (t r)").bitcast(I32))
+        nc.sync.dma_start(csum_col[:], csum)
         for lo, hi in ((0, 384), (384, 768), (768, T)):
             nc.sync.dma_start(zp_all[:, lo:hi], zp[:, lo:hi])
-        nc.sync.dma_start(csum_col[:], csum)
 
         w_grouped = pool.tile([P, N, PACK], BF16, name="w_grouped", align_bytes=256)
         nc.scalar.copy(w_grouped[:].rearrange("p (c i) j -> p c j i", i=4), w_raw[:].rearrange("p j (c i) -> p c j i", i=4))
 
         zg = pool.tile([P, EARLY], F32, name="zg", align_bytes=256)
-        nc.vector.tensor_copy(zg[:], zp_one[:].indirect(offsets[:, : EARLY // 16]))
-        starts = [min(lo, EARLY - P) for lo in range(0, EARLY, P)]
+        nc.vector.tensor_copy(zg[:], zp_one[:].indirect(offsets[:, LATE // 16 :]))
+        starts = range(0, EARLY, P)
         turned = [psum.tile([P, P], F32, name=f"turned{m}", tag=f"turn{m}") for m in range(len(starts))]
         for m, lo in enumerate(starts):
             nc.tensor.transpose(turned[m][:], zg[:, lo : lo + P], ident[:])
-        zg_cols = [pool.tile([P, 1], F32, name=f"zg_col{m}") for m in range(len(starts))]
+        zg_cols = [late.tile([P, 1], F32, name=f"zg_col{m}", offset=256 * m, align_bytes=256) for m in range(len(starts))]
         for m in range(len(starts)):
             nc.scalar.copy(zg_cols[m][:], turned[m][:, P - 1 :])
         spread = [psum.tile([P, P], F32, name=f"spread{m}", tag=f"spread{m}") for m in range(len(starts))]
@@ -69,10 +70,9 @@ def tile_picked_zeropt_none_p_kernel(tc, x_words, x_scales, zp, csum, w1, offs, 
             nc.tensor.transpose(spread[m][:], zg_cols[m][:].to_broadcast([P, P]), ident[:])
         minus_csum = pool.tile([P, 1], F32, name="minus_csum")
         nc.gpsimd.tensor_scalar(minus_csum[:], csum_col[:], -1.0, None, ALU.mult)
-        zg_all = pool.tile([P, S], F32, name="zg_all", align_bytes=256)
+        zg_all = pool.tile([P, EARLY], F32, name="zg_all", align_bytes=256)
         for m, lo in enumerate(starts):
-            done = m * P
-            nc.scalar.activation(zg_all[:, done : lo + P], spread[m][:, done - lo :], COPY)
+            nc.scalar.activation(zg_all[:, lo : lo + P], spread[m][:], COPY)
 
         x_plane = pool.tile([P, S], U8, name="x_plane", align_bytes=256)
         nc.vector.tensor_copy(x_plane[:], planes[:].indirect(offsets[:]))
@@ -83,22 +83,20 @@ def tile_picked_zeropt_none_p_kernel(tc, x_words, x_scales, zp, csum, w1, offs, 
 
         x_codes = shared.tile([P, S], U32, name="x_codes", offset=0, align_bytes=256)
         res = pool.tile([P, S], F32, name="res", align_bytes=256)
-        acc_first = psum.tile([N, HALF], F32, name="acc_first", tag="turn2")
-        acc_mid = psum.tile([N, HALF - LAST], F32, name="acc_mid", tag="spread1")
-        acc_last = psum.tile([N, LAST], F32, name="acc_last", tag="spread2")
-        pieces = ((0, HALF, acc_first), (HALF, S - LAST, acc_mid), (S - LAST, S, acc_last))
-        for group in (pieces[:1], pieces[1:2], pieces[2:]):
-            lo, hi = group[0][0], group[-1][1]
+        firsts = (2 * P, 3 * P, 0, P)
+        accs = [psum.tile([N, P], F32, name=f"acc{lo}", tag=tag) for lo, tag in zip(firsts, ("turn2", "spread0", "spread1", "spread2"))]
+        for lo, acc in zip(firsts, accs):
+            hi = lo + P
             nc.vector.tensor_copy(x_codes[:, lo:hi], words[:].bitcast(U32).indirect(offsets[:, lo // 16 : hi // 16]))
-            for lo, hi, acc in group:
-                nc.tensor.matmul_mx(out=acc[:], lhsT=w_codes[:].bitcast(FP8X4), lhsT_scale=w_plane[:],
-                                    rhs=x_codes[:, lo:hi].bitcast(FP8X4), rhs_scale=x_plane[:, lo:hi], start=True, stop=True)
-        nc.vector.tensor_copy(zg_all[:, EARLY:], zp_all[:].indirect(offsets[:, EARLY // 16 :]))
-        stored = 0
-        for first, last, acc in pieces:
-            for lo in range(first, last, P):
-                hi = lo + P
-                nc.vector.scalar_tensor_tensor(res[:, lo:hi], zg_all[:, lo:hi], minus_csum[:], acc[:, lo - first : hi - first], ALU.mult, ALU.add)
-                if hi <= HALF or hi == S:
-                    nc.sync.dma_start(out[:, stored:hi], res[:, stored:hi])
-                    stored = hi
+            nc.tensor.matmul_mx(out=acc[:], lhsT=w_codes[:].bitcast(FP8X4), lhsT_scale=w_plane[:],
+                                rhs=x_codes[:, lo:hi].bitcast(FP8X4), rhs_scale=x_plane[:, lo:hi], start=True, stop=True)
+        zg_late = late.tile([P, LATE], F32, name="zg_late", offset=512, align_bytes=256)
+        nc.scalar.activation(zg_late[:], zp_all[:].indirect(offsets[:, : LATE // 16]), COPY)
+        for lo, acc in zip(firsts, accs):
+            hi = lo + P
+            picked = zg_late[:] if lo < LATE else zg_all[:, lo - LATE : hi - LATE]
+            nc.vector.scalar_tensor_tensor(res[:, lo:hi], picked, minus_csum[:], acc[:], ALU.mult, ALU.add)
+            if hi == S:
+                nc.sync.dma_start(out[:, HALF:], res[:, HALF:])
+            elif hi <= HALF:
+                nc.sync.dma_start(out[:, lo:hi], res[:, lo:hi])

@@ -18,9 +18,10 @@ COPY = mybir.ActivationFunctionType.Copy
 
 P = 128
 PACK = 4
-HALF = S // 2
 EARLY = 384
 LATE = S - EARLY
+BANK = 512
+BANK_BYTES = 4 * BANK
 
 
 def tile_picked_zeropt_none_p_kernel(tc, x_words, x_scales, zp, csum, w1, offs, out):
@@ -50,7 +51,7 @@ def tile_picked_zeropt_none_p_kernel(tc, x_words, x_scales, zp, csum, w1, offs, 
             (nc.scalar if q == 0 else nc.sync).dma_start(planes[32 * q : 32 * q + 4, :].bitcast(I32), x_scales[0, 4 * q : 4 * q + 4, :].bitcast(I32))
         nc.sync.dma_start(words[:], x_words[0].rearrange("p t r -> p (t r)").bitcast(I32))
         nc.sync.dma_start(csum_col[:], csum)
-        for lo, hi in ((0, 384), (384, 768), (768, T)):
+        for lo, hi in ((0, T // 2), (T // 2, T)):
             nc.sync.dma_start(zp_all[:, lo:hi], zp[:, lo:hi])
 
         w_grouped = pool.tile([P, N, PACK], BF16, name="w_grouped", align_bytes=256)
@@ -59,13 +60,13 @@ def tile_picked_zeropt_none_p_kernel(tc, x_words, x_scales, zp, csum, w1, offs, 
         zg = pool.tile([P, EARLY], F32, name="zg", align_bytes=256)
         nc.vector.tensor_copy(zg[:], zp_one[:].indirect(offsets[:, LATE // 16 :]))
         starts = range(0, EARLY, P)
-        turned = [psum.tile([P, P], F32, name=f"turned{m}", tag=f"turn{m}") for m in range(len(starts))]
+        turned = [psum.tile([P, columns], F32, name=f"turned{m}", offset=m * BANK_BYTES)[:, :P] for m, columns in enumerate((P, P, 2 * BANK))]
         for m, lo in enumerate(starts):
-            nc.tensor.transpose(turned[m][:], zg[:, lo : lo + P], ident[:])
+            nc.tensor.transpose(turned[m], zg[:, lo : lo + P], ident[:])
         zg_cols = [late.tile([P, 1], F32, name=f"zg_col{m}", offset=256 * m, align_bytes=256) for m in range(len(starts))]
         for m in range(len(starts)):
             nc.scalar.copy(zg_cols[m][:], turned[m][:, P - 1 :])
-        spread = [psum.tile([P, P], F32, name=f"spread{m}", tag=f"spread{m}") for m in range(len(starts))]
+        spread = [psum.tile([P, P], F32, name=f"spread{m}", offset=(4 + m) * BANK_BYTES) for m in range(len(starts))]
         for m in range(len(starts)):
             nc.tensor.transpose(spread[m][:], zg_cols[m][:].to_broadcast([P, P]), ident[:])
         minus_csum = pool.tile([P, 1], F32, name="minus_csum")
@@ -84,19 +85,17 @@ def tile_picked_zeropt_none_p_kernel(tc, x_words, x_scales, zp, csum, w1, offs, 
         x_codes = shared.tile([P, S], U32, name="x_codes", offset=0, align_bytes=256)
         res = pool.tile([P, S], F32, name="res", align_bytes=256)
         firsts = (2 * P, 3 * P, 0, P)
-        accs = [psum.tile([N, P], F32, name=f"acc{lo}", tag=tag) for lo, tag in zip(firsts, ("turn2", "spread0", "spread1", "spread2"))]
-        for lo, acc in zip(firsts, accs):
-            hi = lo + P
-            nc.vector.tensor_copy(x_codes[:, lo:hi], words[:].bitcast(U32).indirect(offsets[:, lo // 16 : hi // 16]))
-            nc.tensor.matmul_mx(out=acc[:], lhsT=w_codes[:].bitcast(FP8X4), lhsT_scale=w_plane[:],
-                                rhs=x_codes[:, lo:hi].bitcast(FP8X4), rhs_scale=x_plane[:, lo:hi], start=True, stop=True)
+        accs = [psum.tile([N, P], F32, name=f"acc{lo}", offset=bank * BANK_BYTES) for lo, bank in zip(firsts, (2, 3, 4, 6))]
+        for first, last in ((2 * P, S), (0, P), (P, 2 * P)):
+            nc.vector.tensor_copy(x_codes[:, first:last], words[:].bitcast(U32).indirect(offsets[:, first // 16 : last // 16]))
+            for lo in range(first, last, P):
+                hi = lo + P
+                nc.tensor.matmul_mx(out=accs[firsts.index(lo)][:], lhsT=w_codes[:].bitcast(FP8X4), lhsT_scale=w_plane[:],
+                                    rhs=x_codes[:, lo:hi].bitcast(FP8X4), rhs_scale=x_plane[:, lo:hi], start=True, stop=True)
         zg_late = late.tile([P, LATE], F32, name="zg_late", offset=512, align_bytes=256)
         nc.scalar.activation(zg_late[:], zp_all[:].indirect(offsets[:, : LATE // 16]), COPY)
         for lo, acc in zip(firsts, accs):
             hi = lo + P
             picked = zg_late[:] if lo < LATE else zg_all[:, lo - LATE : hi - LATE]
             nc.vector.scalar_tensor_tensor(res[:, lo:hi], picked, minus_csum[:], acc[:], ALU.mult, ALU.add)
-            if hi == S:
-                nc.sync.dma_start(out[:, HALF:], res[:, HALF:])
-            elif hi <= HALF:
-                nc.sync.dma_start(out[:, lo:hi], res[:, lo:hi])
+            nc.sync.dma_start(out[:, lo:hi], res[:, lo:hi])

@@ -18,8 +18,9 @@ COPY = mybir.ActivationFunctionType.Copy
 
 P = 128
 PACK = 4
-EARLY = 384
+EARLY = 320
 LATE = S - EARLY
+HALF = S // 2
 BANK = 512
 BANK_BYTES = 4 * BANK
 
@@ -59,7 +60,7 @@ def tile_picked_zeropt_none_p_kernel(tc, x_words, x_scales, zp, csum, w1, offs, 
 
         zg = pool.tile([P, EARLY], F32, name="zg", align_bytes=256)
         nc.vector.tensor_copy(zg[:], zp_one[:].indirect(offsets[:, LATE // 16 :]))
-        starts = range(0, EARLY, P)
+        starts = (HALF - LATE, HALF - LATE + P, 0)
         turned = [psum.tile([P, columns], F32, name=f"turned{m}", offset=m * BANK_BYTES)[:, :P] for m, columns in enumerate((P, P, 2 * BANK))]
         for m, lo in enumerate(starts):
             nc.tensor.transpose(turned[m], zg[:, lo : lo + P], ident[:])
@@ -71,9 +72,11 @@ def tile_picked_zeropt_none_p_kernel(tc, x_words, x_scales, zp, csum, w1, offs, 
             nc.tensor.transpose(spread[m][:], zg_cols[m][:].to_broadcast([P, P]), ident[:])
         minus_csum = pool.tile([P, 1], F32, name="minus_csum")
         nc.gpsimd.tensor_scalar(minus_csum[:], csum_col[:], -1.0, None, ALU.mult)
-        zg_all = pool.tile([P, EARLY], F32, name="zg_all", align_bytes=256)
-        for m, lo in enumerate(starts):
-            nc.scalar.activation(zg_all[:, lo : lo + P], spread[m][:], COPY)
+        zg_high = pool.tile([P, HALF], F32, name="zg_high", align_bytes=256)
+        zg_low = late.tile([P, HALF], F32, name="zg_low", offset=512, align_bytes=256)
+        for m in range(2):
+            nc.scalar.activation(zg_high[:, m * P : (m + 1) * P], spread[m][:], COPY)
+        nc.scalar.activation(zg_low[:, LATE:], spread[2][:, : HALF - LATE], COPY)
 
         x_plane = pool.tile([P, S], U8, name="x_plane", align_bytes=256)
         nc.vector.tensor_copy(x_plane[:], planes[:].indirect(offsets[:]))
@@ -92,10 +95,9 @@ def tile_picked_zeropt_none_p_kernel(tc, x_words, x_scales, zp, csum, w1, offs, 
                 hi = lo + P
                 nc.tensor.matmul_mx(out=accs[firsts.index(lo)][:], lhsT=w_codes[:].bitcast(FP8X4), lhsT_scale=w_plane[:],
                                     rhs=x_codes[:, lo:hi].bitcast(FP8X4), rhs_scale=x_plane[:, lo:hi], start=True, stop=True)
-        zg_late = late.tile([P, LATE], F32, name="zg_late", offset=512, align_bytes=256)
-        nc.scalar.activation(zg_late[:], zp_all[:].indirect(offsets[:, : LATE // 16]), COPY)
+        nc.scalar.activation(zg_low[:, :LATE], zp_all[:].indirect(offsets[:, : LATE // 16]), COPY)
         for lo, acc in zip(firsts, accs):
             hi = lo + P
-            picked = zg_late[:] if lo < LATE else zg_all[:, lo - LATE : hi - LATE]
+            picked = zg_low[:, lo:hi] if lo < HALF else zg_high[:, lo - HALF : hi - HALF]
             nc.vector.scalar_tensor_tensor(res[:, lo:hi], picked, minus_csum[:], acc[:], ALU.mult, ALU.add)
             nc.sync.dma_start(out[:, lo:hi], res[:, lo:hi])

from contextlib import ExitStack

import concourse.mybir as mybir
from concourse.masks import make_identity

K, T, S, N = 512, 1024, 512, 128
FLOPS = 2 * K * S * N

F32 = mybir.dt.float32
BF16 = mybir.dt.bfloat16
I32 = mybir.dt.int32
U32 = mybir.dt.uint32
U16 = mybir.dt.uint16
U8 = mybir.dt.uint8
FP8X4 = mybir.dt.float8_e4m3fn_x4
ALU = mybir.AluOpType
COPY = mybir.ActivationFunctionType.Copy

P = 128
PACK = 4
EARLY = 320
LATE = S - EARLY
HALF = S // 2
BANK = 512
BANK_BYTES = 4 * BANK


def tile_picked_zeropt_none_p_kernel(tc, x_words, x_scales, zp, csum, w1, offs, out):
    nc = tc.nc
    with ExitStack() as ctx:
        pool = ctx.enter_context(tc.tile_pool(name="held", bufs=1))
        shared = ctx.enter_context(tc.tile_pool(name="shared", bufs=1))
        late = ctx.enter_context(tc.tile_pool(name="late", bufs=1))
        psum = ctx.enter_context(tc.psum_pool(name="psum", bufs=1))

        offsets = pool.tile([P, S // 16], U16, name="offsets", align_bytes=256)
        words = pool.tile([P, T], I32, name="words", align_bytes=256)
        planes = pool.tile([P, T], U8, name="planes", align_bytes=256)
        zp_one = pool.tile([P, T], F32, name="zp_one", align_bytes=256)
        zp_all = pool.tile([P, T], F32, name="zp_all", align_bytes=256)
        w_raw = shared.tile([P, PACK, N], F32, name="w_raw", offset=0, align_bytes=256)
        csum_col = pool.tile([P, 1], F32, name="csum_col")
        ident = pool.tile([P, P], F32, name="ident", align_bytes=256)
        nc.vector.memset(zp_one[: P - 1, :].bitcast(I32), 0)
        nc.gpsimd.memset(planes[:].bitcast(I32), 0)
        make_identity(nc, ident[:])

        nc.sync.dma_start(offsets[:], offs)
        nc.scalar.dma_start(zp_one[P - 1 :, :], zp[0:1, :])
        nc.sync.dma_start(w_raw[:], w1.rearrange("(p j) n -> p j n", j=PACK))
        for q in range(4):
            (nc.scalar if q == 0 else nc.sync).dma_start(planes[32 * q : 32 * q + 4, :].bitcast(I32), x_scales[0, 4 * q : 4 * q + 4, :].bitcast(I32))
        nc.sync.dma_start(words[:], x_words[0].rearrange("p t r -> p (t r)").bitcast(I32))
        nc.sync.dma_start(csum_col[:], csum)
        for lo, hi in ((0, T // 2), (T // 2, T)):
            nc.sync.dma_start(zp_all[:, lo:hi], zp[:, lo:hi])

        w_grouped = pool.tile([P, N, PACK], BF16, name="w_grouped", align_bytes=256)
        nc.scalar.copy(w_grouped[:].rearrange("p (c i) j -> p c j i", i=4), w_raw[:].rearrange("p j (c i) -> p c j i", i=4))

        zg = pool.tile([P, EARLY], F32, name="zg", align_bytes=256)
        nc.vector.tensor_copy(zg[:], zp_one[:].indirect(offsets[:, LATE // 16 :]))
        starts = (HALF - LATE, HALF - LATE + P, 0)
        turned = [psum.tile([P, columns], F32, name=f"turned{m}", offset=m * BANK_BYTES)[:, :P] for m, columns in enumerate((P, P, 2 * BANK))]
        for m, lo in enumerate(starts):
            nc.tensor.transpose(turned[m], zg[:, lo : lo + P], ident[:])
        zg_cols = [late.tile([P, 1], F32, name=f"zg_col{m}", offset=256 * m, align_bytes=256) for m in range(len(starts))]
        for m in range(len(starts)):
            nc.scalar.copy(zg_cols[m][:], turned[m][:, P - 1 :])
        spread = [psum.tile([P, P], F32, name=f"spread{m}", offset=(4 + m) * BANK_BYTES) for m in range(len(starts))]
        for m in range(len(starts)):
            nc.tensor.transpose(spread[m][:], zg_cols[m][:].to_broadcast([P, P]), ident[:])
        minus_csum = pool.tile([P, 1], F32, name="minus_csum")
        nc.gpsimd.tensor_scalar(minus_csum[:], csum_col[:], -1.0, None, ALU.mult)
        zg_high = pool.tile([P, HALF], F32, name="zg_high", align_bytes=256)
        zg_low = late.tile([P, HALF], F32, name="zg_low", offset=512, align_bytes=256)
        for m in range(2):
            nc.scalar.activation(zg_high[:, m * P : (m + 1) * P], spread[m][:], COPY)
        nc.scalar.activation(zg_low[:, LATE:], spread[2][:, : HALF - LATE], COPY)

        x_plane = pool.tile([P, S], U8, name="x_plane", align_bytes=256)
        nc.vector.tensor_copy(x_plane[:], planes[:].indirect(offsets[:]))

        w_codes = pool.tile([P, N], U32, name="w_codes", align_bytes=256)
        w_plane = pool.tile([P, N], U8, name="w_plane", align_bytes=256)
        nc.vector.quantize_mx(out=w_codes[:].bitcast(FP8X4), scales=w_plane[:], in_=w_grouped[:].rearrange("p n j -> p (n j)"))

        x_codes = shared.tile([P, S], U32, name="x_codes", offset=0, align_bytes=256)
        res = pool.tile([P, S], F32, name="res", align_bytes=256)
        firsts = (2 * P, 3 * P, 0, P)
        accs = [psum.tile([N, P], F32, name=f"acc{lo}", offset=bank * BANK_BYTES) for lo, bank in zip(firsts, (2, 3, 4, 6))]
        for first, last in ((2 * P, S), (0, P), (P, 2 * P)):
            nc.vector.tensor_copy(x_codes[:, first:last], words[:].bitcast(U32).indirect(offsets[:, first // 16 : last // 16]))
            for lo in range(first, last, P):
                hi = lo + P
                nc.tensor.matmul_mx(out=accs[firsts.index(lo)][:], lhsT=w_codes[:].bitcast(FP8X4), lhsT_scale=w_plane[:],
                                    rhs=x_codes[:, lo:hi].bitcast(FP8X4), rhs_scale=x_plane[:, lo:hi], start=True, stop=True)
        nc.scalar.activation(zg_low[:, :LATE], zp_all[:].indirect(offsets[:, : LATE // 16]), COPY)
        for lo, acc in zip(firsts, accs):
            hi = lo + P
            picked = zg_low[:, lo:hi] if lo < HALF else zg_high[:, lo - HALF : hi - HALF]
            nc.vector.scalar_tensor_tensor(res[:, lo:hi], picked, minus_csum[:], acc[:], ALU.mult, ALU.add)
            nc.sync.dma_start(out[:, lo:hi], res[:, lo:hi])
